import numpy as np
import ml_dtypes


def mxq(x, axis, fmt="e4m3"):
    dtype, down = {"e4m3": (ml_dtypes.float8_e4m3fn, 7), "e5m2": (ml_dtypes.float8_e5m2, 14)}[fmt]
    v = np.moveaxis(np.asarray(x, np.float32).astype(ml_dtypes.bfloat16).astype(np.float64), axis, -1)
    blocks = v.reshape(v.shape[:-1] + (-1, 32))
    amax = np.abs(blocks).max(-1, keepdims=True)
    byte = np.maximum(np.where(amax > 0, np.frexp(amax)[1] - 1 + 127, 0) - down, 1)
    scale = np.exp2(byte - 127.0)
    codes = (blocks / scale).astype(np.float32).astype(dtype).astype(np.float64)
    return np.moveaxis((codes * scale).reshape(v.shape), -1, axis)


WIDE = False


def mx_kscale(k):
    if not WIDE:
        return np.ones(k)
    levels = np.array([10, -10, 5, -5, 0])
    if k % 512:
        return np.exp2(np.random.permutation(np.resize(levels, k // 32))).repeat(32)
    a = np.empty((k // 512, 16))
    for p in range(k // 512):
        a[p, :8] = np.random.permutation(np.resize(levels, 8))
        for g in range(8):
            far = levels[np.abs(levels - a[p, g]) >= 10]
            a[p, g + 8] = far[np.random.randint(len(far))]
    return np.exp2(a.ravel()).repeat(32)


def f64(x):
    return np.asarray(x).astype(np.float64)


def striped(idx):
    return np.tile(idx.reshape(-1, 16).T, (8, 1)).astype(np.uint16)


def unstriped(offs):
    return offs[:16].T.reshape(-1).astype(np.int64)


def pack_weight(w):
    k, n = w.shape
    w = f64(np.asarray(w, np.float32).astype(ml_dtypes.bfloat16)).reshape(k // 32, 32, n)
    amax = np.abs(w).max(1)
    byte = np.clip(np.where(amax > 0, np.frexp(amax)[1] - 1 + 127 - 7, 1), 1, 254)
    scaled = (w * np.exp2(127.0 - byte)[:, None, :]).reshape(k, n).astype(np.float32)
    words = np.ascontiguousarray(scaled.reshape(k // 512, 128, 4, n).transpose(0, 1, 3, 2)).astype(ml_dtypes.float8_e4m3fn).view(np.uint8)
    return words, np.ascontiguousarray(byte.astype(np.uint8).reshape(k // 512, 16, n))


def unpack_weight(words, scales):
    g, p, n, _ = words.shape
    vals = np.ascontiguousarray(words).view(ml_dtypes.float8_e4m3fn).astype(np.float64) * np.repeat(np.exp2(scales.astype(np.float64) - 127.0), 8, axis=1)[..., None]
    return vals.transpose(0, 1, 3, 2).reshape(g * 512, n)


def planes(y):
    n, m = y.shape
    v = y.astype(np.float32).astype(ml_dtypes.bfloat16).astype(np.float64).reshape(n // 32, 32, m)
    top = np.abs(v).max(1)
    byte = np.clip(np.where(top > 0, np.frexp(top)[1] - 1 + 127 - 7, 1), 1, 254)
    codes = (v * np.exp2(127.0 - byte)[:, None, :]).reshape(n, m).astype(np.float32).astype(ml_dtypes.float8_e4m3fn).view(np.uint8)
    words = codes.reshape(n // 512, 128, 4, m).transpose(0, 1, 3, 2)
    return np.ascontiguousarray(words), np.ascontiguousarray(byte.astype(np.uint8).reshape(n // 512, 16, m))


K, T, S, N = 1024, 1024, 512, 512
P = 2 ** 7


def setup_inputs():
    n = np.random.standard_normal
    s = mx_kscale(K)[:, None]
    packed_xT = pack_weight(n((K, T)) * s)
    return {
        "x_words": packed_xT[0],
        "x_scales": packed_xT[1],
        "wc0": (n((K, N)) / np.sqrt(K) / s).astype(np.float32),
        "wd0": (n((K, N)) / np.sqrt(K) / s).astype(np.float32),
        "ideal0": (np.tile(np.random.uniform(0.1, 0.6, S), (P, 1))).astype(np.float32),
        "wc1": (n((K, N)) / np.sqrt(K) / s).astype(np.float32),
        "wd1": (n((K, N)) / np.sqrt(K) / s).astype(np.float32),
        "ideal1": (np.tile(np.random.uniform(0.1, 0.6, S), (P, 1))).astype(np.float32),
        "wc2": (n((K, N)) / np.sqrt(K) / s).astype(np.float32),
        "wd2": (n((K, N)) / np.sqrt(K) / s).astype(np.float32),
        "ideal2": (np.tile(np.random.uniform(0.1, 0.6, S), (P, 1))).astype(np.float32),
        "offs": striped(np.random.permutation(T)[:S]),
    }


def reference(x_words, x_scales, wc0, wd0, ideal0, wc1, wd1, ideal1, wc2, wd2, ideal2, offs):
    xq = unpack_weight(x_words, x_scales)[:, unstriped(offs)]
    rec0 = mxq(f64(wc0), 0, "e4m3").T @ xq
    a0 = f64(ideal0)[:1] / ((((mxq(f64(wd0), 0, "e4m3").T @ xq)) ** 2 + 0.3) ** 2)
    rec1 = mxq(f64(wc1), 0, "e4m3").T @ xq
    a1 = f64(ideal1)[:1] / ((((mxq(f64(wd1), 0, "e4m3").T @ xq)) ** 2 + 0.3) ** 2)
    rec2 = mxq(f64(wc2), 0, "e4m3").T @ xq
    a2 = f64(ideal2)[:1] / ((((mxq(f64(wd2), 0, "e4m3").T @ xq)) ** 2 + 0.3) ** 2)
    num = rec0 * a0 + rec1 * a1 + rec2 * a2
    den = a0 + a1 + a2
    out_0 = num / den
    return (out_0,) + planes(out_0)

@@ -1,0 +1,239 @@
+from contextlib import ExitStack
+
+import concourse.mybir as mybir
+from concourse.masks import make_identity
+
+F32 = mybir.dt.float32
+BF16 = mybir.dt.bfloat16
+I32 = mybir.dt.int32
+U32 = mybir.dt.uint32
+U16 = mybir.dt.uint16
+U8 = mybir.dt.uint8
+FP8X4 = mybir.dt.float8_e4m3fn_x4
+ACT = mybir.ActivationFunctionType
+ALU = mybir.AluOpType
+
+K, T, S, N = 1024, 1024, 512, 512
+P = 128
+PACK = 4
+PASSES = K // (P * PACK)
+CANDS = 3
+BLOCKS = S // P
+EPS = 0.3
+FLOPS = 2 * 6 * K * S * N
+
+SCALAR_COLS = [384,384,0,0,0,0,0,0,0,0,512,448]
+
+
+def tile_picked_yweno_rec_po_kernel(
+    tc, x_words, x_scales, wc0, wd0, ideal0, wc1, wd1, ideal1, wc2, wd2, ideal2, offs, out_0, out_1, out_2
+):
+    nc = tc.nc
+    with ExitStack() as ctx:
+        keep = ctx.enter_context(tc.tile_pool(name="keep", bufs=1))
+        ring = ctx.enter_context(tc.tile_pool(name="ring", bufs=3))
+        stage = ctx.enter_context(tc.tile_pool(name="stage", bufs=8))
+        prod_psum = ctx.enter_context(tc.psum_pool(name="prod", bufs=5))
+        sum_psum = ctx.enter_context(tc.psum_pool(name="sums", bufs=3))
+
+        warm = keep.tile([P, 1], F32, name="warm")
+        nc.vector.memset(warm[:], 1.0)
+        warm_out = keep.tile([P, 1], F32, name="warm_out")
+        nc.scalar.activation(warm_out[:], warm[:], ACT.Abs_reciprocal_sqrt)
+
+        offsets = keep.tile([P, S // 16], U16, name="offsets")
+        nc.sync.dma_start(offsets[:], offs)
+
+        table_scales = keep.tile([P, T], U8, name="table_scales", align_bytes=64)
+        nc.vector.memset(table_scales[:].bitcast(I32), 0)
+        ideal_rows = keep.tile([P, P], F32, name="ideal_rows")
+        nc.gpsimd.memset(ideal_rows[:], 0.0)
+        identity = keep.tile([P, P], F32, name="identity")
+        make_identity(nc, identity[:])
+
+        weights = [wd0, wd1, wd2, wc0, wc1, wc2]
+        raw = {}
+
+        def load_weight(w, g):
+            raw[w, g] = stage.tile([P, PACK, N], F32, name="raw")
+            rows = weights[w][g * P * PACK : (g + 1) * P * PACK, :]
+            nc.sync.dma_start(out=raw[w, g][:], in_=rows.rearrange("(p j) n -> p j n", j=PACK))
+
+        table_words = [keep.tile([P, T], U32, name="table_words_%d" % g, align_bytes=64) for g in range(PASSES)]
+
+        def load_words(g):
+            nc.sync.dma_start(
+                out=table_words[g][:].bitcast(I32), in_=x_words[g].rearrange("p n t -> p (n t)").bitcast(I32)
+            )
+
+        load_weight(0, 0)
+        load_words(0)
+        for quad in range(4):
+            nc.sync.dma_start(
+                out=table_scales[32 * quad : 32 * quad + 4 * PASSES, :].bitcast(I32),
+                in_=x_scales[:, 4 * quad : 4 * quad + 4, :].bitcast(I32),
+            )
+        load_words(1)
+        load_weight(0, 1)
+        load_weight(1, 0)
+        for i, ideal in enumerate((ideal0, ideal1, ideal2)):
+            nc.sync.dma_start(
+                out=ideal_rows[BLOCKS * i : BLOCKS * (i + 1), :],
+                in_=ideal[0:1, :].rearrange("o (c j) -> (o c) j", j=P),
+            )
+        load_weight(1, 1)
+        for w in range(2, 6):
+            for g in range(PASSES):
+                load_weight(w, g)
+
+        codes = {}
+        scales = {}
+
+        def interleave(dst, src, split):
+            width = src.shape[2]
+            if split > 0:
+                nc.scalar.copy(
+                    out=dst[:, 0:split, :].rearrange("p (c i) t -> p c t i", i=4),
+                    in_=src[:, :, 0:split].rearrange("p t (c i) -> p c t i", i=4),
+                )
+            if split < width:
+                nc.vector.tensor_copy(
+                    out=dst[:, split:width, :].rearrange("p (c i) t -> p c t i", i=4),
+                    in_=src[:, :, split:width].rearrange("p t (c i) -> p c t i", i=4),
+                )
+
+        rounded = {}
+
+        def round_weight(w, g):
+            rounded[w, g] = ring.tile([P, N, PACK], BF16, name="rounded", align_bytes=64)
+            interleave(rounded[w, g], raw[w, g], SCALAR_COLS[2 * w + g])
+
+        def quantize_weight(w, g):
+            codes[w, g] = keep.tile([P, N], U32, name="codes_%d_%d" % (w, g), align_bytes=64)
+            scales[w, g] = keep.tile([P, N], U8, name="scales_%d_%d" % (w, g), align_bytes=64)
+            nc.vector.quantize_mx(
+                out=codes[w, g][:].bitcast(FP8X4),
+                scales=scales[w, g][:],
+                in_=rounded[w, g][:].rearrange("p n t -> p (n t)"),
+            )
+
+        picked_words = [keep.tile([P, S], U32, name="picked_words_%d" % g, align_bytes=64) for g in range(PASSES)]
+        picked_scales = keep.tile([P, S], U8, name="picked_scales", align_bytes=64)
+
+        def product(w, c):
+            bank = prod_psum.tile([P, N], F32, name="product")
+            cols = slice(c * P, (c + 1) * P)
+            for g in range(PASSES):
+                nc.tensor.matmul_mx(
+                    out=bank[:],
+                    lhsT=picked_words[g][:, cols].bitcast(FP8X4),
+                    lhsT_scale=picked_scales[4 * g : P, cols],
+                    rhs=codes[w, g][:].bitcast(FP8X4),
+                    rhs_scale=scales[w, g][:],
+                    start=(g == 0),
+                    stop=(g == PASSES - 1),
+                )
+            return bank[:].rearrange("j (p t) -> j t p", t=PACK)
+
+        def turned_sum(terms):
+            bank = sum_psum.tile([P, PACK, P], F32, name="turned")
+            for t in range(PACK):
+                for i, term in enumerate(terms):
+                    nc.tensor.matmul(
+                        bank[:, t, :], term[:, t, :], identity[:],
+                        start=(i == 0), stop=(i == len(terms) - 1), is_transpose=True,
+                    )
+            return bank
+
+        round_weight(0, 0)
+        nc.vector.tensor_copy(picked_words[0][:], table_words[0][:].indirect(offsets[:]))
+        quantize_weight(0, 0)
+        nc.vector.tensor_copy(picked_scales[:], table_scales[:].indirect(offsets[:]))
+        nc.vector.tensor_copy(picked_words[1][:], table_words[1][:].indirect(offsets[:]))
+        round_weight(0, 1)
+        quantize_weight(0, 1)
+
+        ideal_bank = sum_psum.tile([P, PACK, P], F32, name="turned")
+        nc.tensor.transpose(ideal_bank[:, 0, :], ideal_rows[:], identity[:])
+        ideal_cols = keep.tile([P, 16], F32, name="ideal_cols")
+        nc.vector.tensor_copy(ideal_cols[:], ideal_bank[:, 0, 0:16])
+
+        alpha = {}
+        term = {}
+        inv_den = {}
+
+        def smooth(i, c):
+            d = product(i, c)
+            sq = ring.tile([P, PACK, P], F32, name="sq")
+            nc.scalar.activation(sq[:], d, ACT.Square)
+            q = ring.tile([P, PACK, P], F32, name="q")
+            nc.scalar.activation(q[:], sq[:], ACT.Square, bias=EPS)
+            v = ring.tile([P, N], F32, name="v")
+            nc.scalar.activation(v[:], q[:].rearrange("j t p -> j (t p)"), ACT.Abs_reciprocal_sqrt)
+            alpha[i, c] = keep.tile([P, PACK, P], F32, name="alpha_%d_%d" % (i, c))
+            col = BLOCKS * i + c
+            nc.vector.scalar_tensor_tensor(
+                alpha[i, c][:].rearrange("j t p -> j (t p)"), v[:], ideal_cols[:, col : col + 1], v[:],
+                ALU.mult, ALU.mult,
+            )
+
+        def weigh(i, c):
+            rec = product(CANDS + i, c)
+            term[i, c] = keep.tile([P, PACK, P], F32, name="term_%d_%d" % (i, c))
+            nc.vector.tensor_tensor(term[i, c][:], rec, alpha[i, c][:], ALU.mult)
+
+        def invert(c):
+            den = turned_sum([alpha[i, c] for i in range(CANDS)])
+            root = ring.tile([P, PACK, P], F32, name="root")
+            nc.scalar.activation(root[:], den[:], ACT.Abs_reciprocal_sqrt)
+            sgn = ring.tile([P, PACK, P], F32, name="sgn")
+            nc.scalar.activation(sgn[:], den[:], ACT.Sign)
+            mag = ring.tile([P, PACK, P], F32, name="mag")
+            nc.scalar.activation(mag[:], root[:], ACT.Square)
+            inv_den[c] = keep.tile([P, PACK, P], F32, name="inv_den_%d" % c)
+            nc.vector.tensor_tensor(inv_den[c][:], mag[:], sgn[:], ALU.mult)
+
+        out_words = keep.tile([P, S], U32, name="out_words", align_bytes=64)
+        out_scales = keep.tile([P, S], U8, name="out_scales", align_bytes=64)
+        out_rows = out_0.rearrange("(p t) j -> p t j", t=PACK)
+        words_dram = out_1[0].rearrange("p n t -> p (n t)").bitcast(I32)
+
+        def finish(c):
+            cols = slice(c * P, (c + 1) * P)
+            num = turned_sum([term[i, c] for i in range(CANDS)])
+            y = keep.tile([P, PACK, P], F32, name="y_%d" % c)
+            nc.vector.tensor_tensor(y[:], num[:], inv_den[c][:], ALU.mult)
+            nc.sync.dma_start(out=out_rows[:, :, cols], in_=y[:])
+            y_rounded = keep.tile([P, P, PACK], BF16, name="y_rounded_%d" % c, align_bytes=64)
+            interleave(y_rounded, y, P)
+            nc.vector.quantize_mx(
+                out=out_words[:, cols].bitcast(FP8X4),
+                scales=out_scales[:, cols],
+                in_=y_rounded[:].rearrange("p n t -> p (n t)"),
+            )
+
+        def prepare(w):
+            for g in range(PASSES):
+                round_weight(w, g)
+                quantize_weight(w, g)
+
+        for i in range(CANDS):
+            prepare(i + 1)
+            for c in range(BLOCKS):
+                smooth(i, c)
+        for i in range(CANDS - 1):
+            prepare(CANDS + i + 1)
+            for c in range(BLOCKS):
+                weigh(i, c)
+        for c in range(BLOCKS):
+            invert(c)
+        for c in range(BLOCKS):
+            weigh(CANDS - 1, c)
+            finish(c)
+        nc.sync.dma_start(out=words_dram, in_=out_words[:].bitcast(I32))
+        for quad in range(4):
+            queue = nc.scalar if quad % 2 else nc.sync
+            queue.dma_start(
+                out=out_2[0, 4 * quad : 4 * quad + 4, :].bitcast(I32),
+                in_=out_scales[32 * quad : 32 * quad + 4, :].bitcast(I32),
+            )

@@ -20,9 +20,11 @@ PASSES = K // (P * PACK)
 CANDS = 3
 BLOCKS = S // P
 EPS = 0.3
+HALF = N // 2
+HEAD_COLS = [256,128,0,0]
 FLOPS = 2 * 6 * K * S * N
 
-SCALAR_COLS = [384,384,0,0,0,0,0,0,0,0,512,448]
+SCALAR_COLS = [0,0,0,0,0,0,0,0,0,512,512,512]
 
 
 def tile_picked_yweno_rec_po_kernel(
@@ -32,9 +34,9 @@ def tile_picked_yweno_rec_po_kernel(
     with ExitStack() as ctx:
         keep = ctx.enter_context(tc.tile_pool(name="keep", bufs=1))
         ring = ctx.enter_context(tc.tile_pool(name="ring", bufs=3))
-        stage = ctx.enter_context(tc.tile_pool(name="stage", bufs=8))
-        prod_psum = ctx.enter_context(tc.psum_pool(name="prod", bufs=5))
-        sum_psum = ctx.enter_context(tc.psum_pool(name="sums", bufs=3))
+        stage = ctx.enter_context(tc.tile_pool(name="stage", bufs=6))
+        prod_psum = ctx.enter_context(tc.psum_pool(name="prod", bufs=4))
+        sum_psum = ctx.enter_context(tc.psum_pool(name="sums", bufs=4))
 
         warm = keep.tile([P, 1], F32, name="warm")
         nc.vector.memset(warm[:], 1.0)
@@ -66,15 +68,24 @@ def tile_picked_yweno_rec_po_kernel(
                 out=table_words[g][:].bitcast(I32), in_=x_words[g].rearrange("p n t -> p (n t)").bitcast(I32)
             )
 
-        load_weight(0, 0)
+        half_raw = {}
+
+        def load_half(u, g):
+            half_raw[u, g] = keep.tile([P, PACK, HALF], F32, name="half_raw_%d_%d" % (u, g))
+            rows = wd0[g * P * PACK : (g + 1) * P * PACK, u * HALF : (u + 1) * HALF]
+            nc.sync.dma_start(out=half_raw[u, g][:], in_=rows.rearrange("(p j) n -> p j n", j=PACK))
+
         load_words(0)
         for quad in range(4):
             nc.sync.dma_start(
                 out=table_scales[32 * quad : 32 * quad + 4 * PASSES, :].bitcast(I32),
                 in_=x_scales[:, 4 * quad : 4 * quad + 4, :].bitcast(I32),
             )
+        load_half(0, 0)
         load_words(1)
-        load_weight(0, 1)
+        load_half(0, 1)
+        load_half(1, 0)
+        load_half(1, 1)
         load_weight(1, 0)
         for i, ideal in enumerate((ideal0, ideal1, ideal2)):
             nc.sync.dma_start(
@@ -103,9 +114,15 @@ def tile_picked_yweno_rec_po_kernel(
                 )
 
         rounded = {}
+        both = {}
 
         def round_weight(w, g):
-            rounded[w, g] = ring.tile([P, N, PACK], BF16, name="rounded", align_bytes=64)
+            if 2 <= w < 2 + CANDS:
+                if g == 0:
+                    both[w] = keep.tile([P, PASSES, N, PACK], BF16, name="shared_%d" % (w - 2), align_bytes=64)
+                rounded[w, g] = both[w][:, g]
+            else:
+                rounded[w, g] = ring.tile([P, N, PACK], BF16, name="rounded", align_bytes=64)
             interleave(rounded[w, g], raw[w, g], SCALAR_COLS[2 * w + g])
 
         def quantize_weight(w, g):
@@ -135,60 +152,128 @@ def tile_picked_yweno_rec_po_kernel(
                 )
             return bank[:].rearrange("j (p t) -> j t p", t=PACK)
 
-        def turned_sum(terms):
-            bank = sum_psum.tile([P, PACK, P], F32, name="turned")
+        def add_turned(bank, addend, i):
             for t in range(PACK):
-                for i, term in enumerate(terms):
-                    nc.tensor.matmul(
-                        bank[:, t, :], term[:, t, :], identity[:],
-                        start=(i == 0), stop=(i == len(terms) - 1), is_transpose=True,
-                    )
-            return bank
+                nc.tensor.matmul(
+                    bank[:, t, :], addend[:, t, :], identity[:],
+                    start=(i == 0 and t == 0), stop=(i == CANDS - 1 and t == PACK - 1), is_transpose=True,
+                )
 
-        round_weight(0, 0)
+        half_rounded = {}
+        half_codes = {}
+        half_scales = {}
+
+        def round_half(u, g):
+            half_rounded[u, g] = ring.tile([P, HALF, PACK], BF16, name="rounded", align_bytes=64)
+            interleave(half_rounded[u, g], half_raw[u, g], HEAD_COLS[2 * u + g])
+
+        def quantize_half(u, g):
+            half_codes[u, g] = keep.tile([P, HALF], U32, name="half_codes_%d_%d" % (u, g), align_bytes=64)
+            half_scales[u, g] = keep.tile([P, HALF], U8, name="half_scales_%d_%d" % (u, g), align_bytes=64)
+            nc.vector.quantize_mx(
+                out=half_codes[u, g][:].bitcast(FP8X4),
+                scales=half_scales[u, g][:],
+                in_=half_rounded[u, g][:].rearrange("p n t -> p (n t)"),
+            )
+
         nc.vector.tensor_copy(picked_words[0][:], table_words[0][:].indirect(offsets[:]))
-        quantize_weight(0, 0)
         nc.vector.tensor_copy(picked_scales[:], table_scales[:].indirect(offsets[:]))
+        round_half(0, 0)
         nc.vector.tensor_copy(picked_words[1][:], table_words[1][:].indirect(offsets[:]))
-        round_weight(0, 1)
-        quantize_weight(0, 1)
+        quantize_half(0, 0)
+        round_half(0, 1)
+        quantize_half(0, 1)
+        round_half(1, 0)
+        round_half(1, 1)
+        quantize_half(1, 0)
+        quantize_half(1, 1)
 
         ideal_bank = sum_psum.tile([P, PACK, P], F32, name="turned")
         nc.tensor.transpose(ideal_bank[:, 0, :], ideal_rows[:], identity[:])
         ideal_cols = keep.tile([P, 16], F32, name="ideal_cols")
         nc.vector.tensor_copy(ideal_cols[:], ideal_bank[:, 0, 0:16])
 
+        inv_smooth = {}
         alpha = {}
-        term = {}
+        alpha_all = {}
+        den_bank = {}
+        num_bank = {}
         inv_den = {}
+        pairs = range(BLOCKS // 2)
 
-        def smooth(i, c):
-            d = product(i, c)
-            sq = ring.tile([P, PACK, P], F32, name="sq")
-            nc.scalar.activation(sq[:], d, ACT.Square)
-            q = ring.tile([P, PACK, P], F32, name="q")
-            nc.scalar.activation(q[:], sq[:], ACT.Square, bias=EPS)
-            v = ring.tile([P, N], F32, name="v")
-            nc.scalar.activation(v[:], q[:].rearrange("j t p -> j (t p)"), ACT.Abs_reciprocal_sqrt)
-            alpha[i, c] = keep.tile([P, PACK, P], F32, name="alpha_%d_%d" % (i, c))
+        def smooth_first():
+            whole = keep.tile([P, BLOCKS, PACK, P], F32, name="inv_smooth_0")
+            for u in range(2):
+                sq = ring.tile([P, BLOCKS, PACK, P // 2], F32, name="sq", bufs=2)
+                for h in pairs:
+                    bank = prod_psum.tile([P, 2, HALF], F32, name="product")
+                    for e in range(2):
+                        cols = slice((2 * h + e) * P, (2 * h + e + 1) * P)
+                        for g in range(PASSES):
+                            nc.tensor.matmul_mx(
+                                out=bank[:, e, :],
+                                lhsT=picked_words[g][:, cols].bitcast(FP8X4),
+                                lhsT_scale=picked_scales[4 * g : P, cols],
+                                rhs=half_codes[u, g][:].bitcast(FP8X4),
+                                rhs_scale=half_scales[u, g][:],
+                                start=(g == 0),
+                                stop=(g == PASSES - 1),
+                            )
+                    nc.scalar.activation(
+                        sq[:, 2 * h : 2 * h + 2], bank[:].rearrange("j e (p t) -> j e t p", t=PACK), ACT.Square
+                    )
+                rough = ring.tile([P, BLOCKS, PACK, P // 2], F32, name="rough", bufs=2)
+                nc.scalar.activation(rough[:], sq[:], ACT.Square, bias=EPS)
+                nc.scalar.activation(
+                    whole[:, :, :, u * (P // 2) : (u + 1) * (P // 2)], rough[:], ACT.Abs_reciprocal_sqrt
+                )
+            for c in range(BLOCKS):
+                inv_smooth[0, c] = whole[:, c].rearrange("j t p -> j (t p)")
+
+        def smooth(i):
+            sq = {}
+            for h in pairs:
+                sq[h] = ring.tile([P, 2, PACK, P], F32, name="sq", bufs=2)
+                for e in range(2):
+                    nc.scalar.activation(sq[h][:, e], product(i, 2 * h + e), ACT.Square)
+            rough = {}
+            for h in pairs:
+                rough[h] = ring.tile([P, 2, N], F32, name="rough", bufs=2)
+                nc.scalar.activation(rough[h][:], sq[h][:].rearrange("j e t p -> j e (t p)"), ACT.Square, bias=EPS)
+            for h in pairs:
+                inv = ring.tile([P, 2, N], F32, name="inv_smooth", bufs=4)
+                nc.scalar.activation(inv[:], rough[h][:], ACT.Abs_reciprocal_sqrt)
+                for e in range(2):
+                    inv_smooth[i, 2 * h + e] = inv[:, e]
+
+        def ratio(i, c):
+            if c == 0:
+                alpha_all[i] = keep.tile([P, BLOCKS, PACK, P], F32, name="shared_%d" % i, align_bytes=64)
+            alpha[i, c] = alpha_all[i][:, c]
             col = BLOCKS * i + c
             nc.vector.scalar_tensor_tensor(
-                alpha[i, c][:].rearrange("j t p -> j (t p)"), v[:], ideal_cols[:, col : col + 1], v[:],
-                ALU.mult, ALU.mult,
+                alpha[i, c][:].rearrange("j t p -> j (t p)"), inv_smooth[i, c], ideal_cols[:, col : col + 1],
+                inv_smooth[i, c], ALU.mult, ALU.mult,
             )
+            if i == 0:
+                den_bank[c] = sum_psum.tile([P, PACK, P], F32, name="turned")
+            add_turned(den_bank[c], alpha[i, c], i)
 
         def weigh(i, c):
             rec = product(CANDS + i, c)
-            term[i, c] = keep.tile([P, PACK, P], F32, name="term_%d_%d" % (i, c))
-            nc.vector.tensor_tensor(term[i, c][:], rec, alpha[i, c][:], ALU.mult)
+            term = ring.tile([P, PACK, P], F32, name="term", bufs=8)
+            nc.vector.tensor_tensor(term[:], rec, alpha[i, c][:], ALU.mult)
+            if i == 0:
+                num_bank[c] = sum_psum.tile([P, PACK, P], F32, name="turned")
+            add_turned(num_bank[c], term, i)
 
         def invert(c):
-            den = turned_sum([alpha[i, c] for i in range(CANDS)])
-            root = ring.tile([P, PACK, P], F32, name="root")
+            den = den_bank[c]
+            root = ring.tile([P, PACK, P], F32, name="root", bufs=2)
             nc.scalar.activation(root[:], den[:], ACT.Abs_reciprocal_sqrt)
-            sgn = ring.tile([P, PACK, P], F32, name="sgn")
+            sgn = ring.tile([P, PACK, P], F32, name="sgn", bufs=2)
             nc.scalar.activation(sgn[:], den[:], ACT.Sign)
-            mag = ring.tile([P, PACK, P], F32, name="mag")
+            mag = ring.tile([P, PACK, P], F32, name="mag", bufs=2)
             nc.scalar.activation(mag[:], root[:], ACT.Square)
             inv_den[c] = keep.tile([P, PACK, P], F32, name="inv_den_%d" % c)
             nc.vector.tensor_tensor(inv_den[c][:], mag[:], sgn[:], ALU.mult)
@@ -200,7 +285,7 @@ def tile_picked_yweno_rec_po_kernel(
 
         def finish(c):
             cols = slice(c * P, (c + 1) * P)
-            num = turned_sum([term[i, c] for i in range(CANDS)])
+            num = num_bank[c]
             y = keep.tile([P, PACK, P], F32, name="y_%d" % c)
             nc.vector.tensor_tensor(y[:], num[:], inv_den[c][:], ALU.mult)
             nc.sync.dma_start(out=out_rows[:, :, cols], in_=y[:])
@@ -215,18 +300,28 @@ def tile_picked_yweno_rec_po_kernel(
         def prepare(w):
             for g in range(PASSES):
                 round_weight(w, g)
+            for g in range(PASSES):
                 quantize_weight(w, g)
 
-        for i in range(CANDS):
-            prepare(i + 1)
-            for c in range(BLOCKS):
-                smooth(i, c)
-        for i in range(CANDS - 1):
-            prepare(CANDS + i + 1)
-            for c in range(BLOCKS):
-                weigh(i, c)
+        prepare(1)
+        smooth_first()
+        prepare(2)
+        smooth(1)
+        for c in range(BLOCKS):
+            ratio(0, c)
+        prepare(3)
+        smooth(2)
+        for c in range(BLOCKS):
+            ratio(1, c)
+        prepare(4)
+        for c in range(BLOCKS):
+            ratio(2, c)
+        prepare(5)
         for c in range(BLOCKS):
             invert(c)
+        for i in range(CANDS - 1):
+            for c in range(BLOCKS):
+                weigh(i, c)
         for c in range(BLOCKS):
             weigh(CANDS - 1, c)
             finish(c)

from contextlib import ExitStack

import concourse.mybir as mybir
from concourse.masks import make_identity

F32 = mybir.dt.float32
BF16 = mybir.dt.bfloat16
I32 = mybir.dt.int32
U32 = mybir.dt.uint32
U16 = mybir.dt.uint16
U8 = mybir.dt.uint8
FP8X4 = mybir.dt.float8_e4m3fn_x4
ACT = mybir.ActivationFunctionType
ALU = mybir.AluOpType

K, T, S, N = 1024, 1024, 512, 512
P = 128
PACK = 4
PASSES = K // (P * PACK)
CANDS = 3
BLOCKS = S // P
EPS = 0.3
HALF = N // 2
HEAD_COLS = [256,128,0,0]
FLOPS = 2 * 6 * K * S * N

SCALAR_COLS = [0,0,0,0,0,0,0,0,0,512,512,512]


def tile_picked_yweno_rec_po_kernel(
    tc, x_words, x_scales, wc0, wd0, ideal0, wc1, wd1, ideal1, wc2, wd2, ideal2, offs, out_0, out_1, out_2
):
    nc = tc.nc
    with ExitStack() as ctx:
        keep = ctx.enter_context(tc.tile_pool(name="keep", bufs=1))
        ring = ctx.enter_context(tc.tile_pool(name="ring", bufs=3))
        stage = ctx.enter_context(tc.tile_pool(name="stage", bufs=6))
        prod_psum = ctx.enter_context(tc.psum_pool(name="prod", bufs=4))
        sum_psum = ctx.enter_context(tc.psum_pool(name="sums", bufs=4))

        warm = keep.tile([P, 1], F32, name="warm")
        nc.vector.memset(warm[:], 1.0)
        warm_out = keep.tile([P, 1], F32, name="warm_out")
        nc.scalar.activation(warm_out[:], warm[:], ACT.Abs_reciprocal_sqrt)

        offsets = keep.tile([P, S // 16], U16, name="offsets")
        nc.sync.dma_start(offsets[:], offs)

        table_scales = keep.tile([P, T], U8, name="table_scales", align_bytes=64)
        nc.vector.memset(table_scales[:].bitcast(I32), 0)
        ideal_rows = keep.tile([P, P], F32, name="ideal_rows")
        nc.gpsimd.memset(ideal_rows[:], 0.0)
        identity = keep.tile([P, P], F32, name="identity")
        make_identity(nc, identity[:])

        weights = [wd0, wd1, wd2, wc0, wc1, wc2]
        raw = {}

        def load_weight(w, g):
            raw[w, g] = stage.tile([P, PACK, N], F32, name="raw")
            rows = weights[w][g * P * PACK : (g + 1) * P * PACK, :]
            nc.sync.dma_start(out=raw[w, g][:], in_=rows.rearrange("(p j) n -> p j n", j=PACK))

        table_words = [keep.tile([P, T], U32, name="table_words_%d" % g, align_bytes=64) for g in range(PASSES)]

        def load_words(g):
            nc.sync.dma_start(
                out=table_words[g][:].bitcast(I32), in_=x_words[g].rearrange("p n t -> p (n t)").bitcast(I32)
            )

        half_raw = {}

        def load_half(u, g):
            half_raw[u, g] = keep.tile([P, PACK, HALF], F32, name="half_raw_%d_%d" % (u, g))
            rows = wd0[g * P * PACK : (g + 1) * P * PACK, u * HALF : (u + 1) * HALF]
            nc.sync.dma_start(out=half_raw[u, g][:], in_=rows.rearrange("(p j) n -> p j n", j=PACK))

        load_words(0)
        for quad in range(4):
            nc.sync.dma_start(
                out=table_scales[32 * quad : 32 * quad + 4 * PASSES, :].bitcast(I32),
                in_=x_scales[:, 4 * quad : 4 * quad + 4, :].bitcast(I32),
            )
        load_half(0, 0)
        load_words(1)
        load_half(0, 1)
        load_half(1, 0)
        load_half(1, 1)
        load_weight(1, 0)
        for i, ideal in enumerate((ideal0, ideal1, ideal2)):
            nc.sync.dma_start(
                out=ideal_rows[BLOCKS * i : BLOCKS * (i + 1), :],
                in_=ideal[0:1, :].rearrange("o (c j) -> (o c) j", j=P),
            )
        load_weight(1, 1)
        for w in range(2, 6):
            for g in range(PASSES):
                load_weight(w, g)

        codes = {}
        scales = {}

        def interleave(dst, src, split):
            width = src.shape[2]
            if split > 0:
                nc.scalar.copy(
                    out=dst[:, 0:split, :].rearrange("p (c i) t -> p c t i", i=4),
                    in_=src[:, :, 0:split].rearrange("p t (c i) -> p c t i", i=4),
                )
            if split < width:
                nc.vector.tensor_copy(
                    out=dst[:, split:width, :].rearrange("p (c i) t -> p c t i", i=4),
                    in_=src[:, :, split:width].rearrange("p t (c i) -> p c t i", i=4),
                )

        rounded = {}
        both = {}

        def round_weight(w, g):
            if 2 <= w < 2 + CANDS:
                if g == 0:
                    both[w] = keep.tile([P, PASSES, N, PACK], BF16, name="shared_%d" % (w - 2), align_bytes=64)
                rounded[w, g] = both[w][:, g]
            else:
                rounded[w, g] = ring.tile([P, N, PACK], BF16, name="rounded", align_bytes=64)
            interleave(rounded[w, g], raw[w, g], SCALAR_COLS[2 * w + g])

        def quantize_weight(w, g):
            codes[w, g] = keep.tile([P, N], U32, name="codes_%d_%d" % (w, g), align_bytes=64)
            scales[w, g] = keep.tile([P, N], U8, name="scales_%d_%d" % (w, g), align_bytes=64)
            nc.vector.quantize_mx(
                out=codes[w, g][:].bitcast(FP8X4),
                scales=scales[w, g][:],
                in_=rounded[w, g][:].rearrange("p n t -> p (n t)"),
            )

        picked_words = [keep.tile([P, S], U32, name="picked_words_%d" % g, align_bytes=64) for g in range(PASSES)]
        picked_scales = keep.tile([P, S], U8, name="picked_scales", align_bytes=64)

        def product(w, c):
            bank = prod_psum.tile([P, N], F32, name="product")
            cols = slice(c * P, (c + 1) * P)
            for g in range(PASSES):
                nc.tensor.matmul_mx(
                    out=bank[:],
                    lhsT=picked_words[g][:, cols].bitcast(FP8X4),
                    lhsT_scale=picked_scales[4 * g : P, cols],
                    rhs=codes[w, g][:].bitcast(FP8X4),
                    rhs_scale=scales[w, g][:],
                    start=(g == 0),
                    stop=(g == PASSES - 1),
                )
            return bank[:].rearrange("j (p t) -> j t p", t=PACK)

        def add_turned(bank, addend, i):
            for t in range(PACK):
                nc.tensor.matmul(
                    bank[:, t, :], addend[:, t, :], identity[:],
                    start=(i == 0 and t == 0), stop=(i == CANDS - 1 and t == PACK - 1), is_transpose=True,
                )

        half_rounded = {}
        half_codes = {}
        half_scales = {}

        def round_half(u, g):
            half_rounded[u, g] = ring.tile([P, HALF, PACK], BF16, name="rounded", align_bytes=64)
            interleave(half_rounded[u, g], half_raw[u, g], HEAD_COLS[2 * u + g])

        def quantize_half(u, g):
            half_codes[u, g] = keep.tile([P, HALF], U32, name="half_codes_%d_%d" % (u, g), align_bytes=64)
            half_scales[u, g] = keep.tile([P, HALF], U8, name="half_scales_%d_%d" % (u, g), align_bytes=64)
            nc.vector.quantize_mx(
                out=half_codes[u, g][:].bitcast(FP8X4),
                scales=half_scales[u, g][:],
                in_=half_rounded[u, g][:].rearrange("p n t -> p (n t)"),
            )

        nc.vector.tensor_copy(picked_words[0][:], table_words[0][:].indirect(offsets[:]))
        nc.vector.tensor_copy(picked_scales[:], table_scales[:].indirect(offsets[:]))
        round_half(0, 0)
        nc.vector.tensor_copy(picked_words[1][:], table_words[1][:].indirect(offsets[:]))
        quantize_half(0, 0)
        round_half(0, 1)
        quantize_half(0, 1)
        round_half(1, 0)
        round_half(1, 1)
        quantize_half(1, 0)
        quantize_half(1, 1)

        ideal_bank = sum_psum.tile([P, PACK, P], F32, name="turned")
        nc.tensor.transpose(ideal_bank[:, 0, :], ideal_rows[:], identity[:])
        ideal_cols = keep.tile([P, 16], F32, name="ideal_cols")
        nc.vector.tensor_copy(ideal_cols[:], ideal_bank[:, 0, 0:16])

        inv_smooth = {}
        alpha = {}
        alpha_all = {}
        den_bank = {}
        num_bank = {}
        inv_den = {}
        pairs = range(BLOCKS // 2)

        def smooth_first():
            whole = keep.tile([P, BLOCKS, PACK, P], F32, name="inv_smooth_0")
            for u in range(2):
                sq = ring.tile([P, BLOCKS, PACK, P // 2], F32, name="sq", bufs=2)
                for h in pairs:
                    bank = prod_psum.tile([P, 2, HALF], F32, name="product")
                    for e in range(2):
                        cols = slice((2 * h + e) * P, (2 * h + e + 1) * P)
                        for g in range(PASSES):
                            nc.tensor.matmul_mx(
                                out=bank[:, e, :],
                                lhsT=picked_words[g][:, cols].bitcast(FP8X4),
                                lhsT_scale=picked_scales[4 * g : P, cols],
                                rhs=half_codes[u, g][:].bitcast(FP8X4),
                                rhs_scale=half_scales[u, g][:],
                                start=(g == 0),
                                stop=(g == PASSES - 1),
                            )
                    nc.scalar.activation(
                        sq[:, 2 * h : 2 * h + 2], bank[:].rearrange("j e (p t) -> j e t p", t=PACK), ACT.Square
                    )
                rough = ring.tile([P, BLOCKS, PACK, P // 2], F32, name="rough", bufs=2)
                nc.scalar.activation(rough[:], sq[:], ACT.Square, bias=EPS)
                nc.scalar.activation(
                    whole[:, :, :, u * (P // 2) : (u + 1) * (P // 2)], rough[:], ACT.Abs_reciprocal_sqrt
                )
            for c in range(BLOCKS):
                inv_smooth[0, c] = whole[:, c].rearrange("j t p -> j (t p)")

        def smooth(i):
            sq = {}
            for h in pairs:
                sq[h] = ring.tile([P, 2, PACK, P], F32, name="sq", bufs=2)
                for e in range(2):
                    nc.scalar.activation(sq[h][:, e], product(i, 2 * h + e), ACT.Square)
            rough = {}
            for h in pairs:
                rough[h] = ring.tile([P, 2, N], F32, name="rough", bufs=2)
                nc.scalar.activation(rough[h][:], sq[h][:].rearrange("j e t p -> j e (t p)"), ACT.Square, bias=EPS)
            for h in pairs:
                inv = ring.tile([P, 2, N], F32, name="inv_smooth", bufs=4)
                nc.scalar.activation(inv[:], rough[h][:], ACT.Abs_reciprocal_sqrt)
                for e in range(2):
                    inv_smooth[i, 2 * h + e] = inv[:, e]

        def ratio(i, c):
            if c == 0:
                alpha_all[i] = keep.tile([P, BLOCKS, PACK, P], F32, name="shared_%d" % i, align_bytes=64)
            alpha[i, c] = alpha_all[i][:, c]
            col = BLOCKS * i + c
            nc.vector.scalar_tensor_tensor(
                alpha[i, c][:].rearrange("j t p -> j (t p)"), inv_smooth[i, c], ideal_cols[:, col : col + 1],
                inv_smooth[i, c], ALU.mult, ALU.mult,
            )
            if i == 0:
                den_bank[c] = sum_psum.tile([P, PACK, P], F32, name="turned")
            add_turned(den_bank[c], alpha[i, c], i)

        def weigh(i, c):
            rec = product(CANDS + i, c)
            term = ring.tile([P, PACK, P], F32, name="term", bufs=8)
            nc.vector.tensor_tensor(term[:], rec, alpha[i, c][:], ALU.mult)
            if i == 0:
                num_bank[c] = sum_psum.tile([P, PACK, P], F32, name="turned")
            add_turned(num_bank[c], term, i)

        def invert(c):
            den = den_bank[c]
            root = ring.tile([P, PACK, P], F32, name="root", bufs=2)
            nc.scalar.activation(root[:], den[:], ACT.Abs_reciprocal_sqrt)
            sgn = ring.tile([P, PACK, P], F32, name="sgn", bufs=2)
            nc.scalar.activation(sgn[:], den[:], ACT.Sign)
            mag = ring.tile([P, PACK, P], F32, name="mag", bufs=2)
            nc.scalar.activation(mag[:], root[:], ACT.Square)
            inv_den[c] = keep.tile([P, PACK, P], F32, name="inv_den_%d" % c)
            nc.vector.tensor_tensor(inv_den[c][:], mag[:], sgn[:], ALU.mult)

        out_words = keep.tile([P, S], U32, name="out_words", align_bytes=64)
        out_scales = keep.tile([P, S], U8, name="out_scales", align_bytes=64)
        out_rows = out_0.rearrange("(p t) j -> p t j", t=PACK)
        words_dram = out_1[0].rearrange("p n t -> p (n t)").bitcast(I32)

        def finish(c):
            cols = slice(c * P, (c + 1) * P)
            num = num_bank[c]
            y = keep.tile([P, PACK, P], F32, name="y_%d" % c)
            nc.vector.tensor_tensor(y[:], num[:], inv_den[c][:], ALU.mult)
            nc.sync.dma_start(out=out_rows[:, :, cols], in_=y[:])
            y_rounded = keep.tile([P, P, PACK], BF16, name="y_rounded_%d" % c, align_bytes=64)
            interleave(y_rounded, y, P)
            nc.vector.quantize_mx(
                out=out_words[:, cols].bitcast(FP8X4),
                scales=out_scales[:, cols],
                in_=y_rounded[:].rearrange("p n t -> p (n t)"),
            )

        def prepare(w):
            for g in range(PASSES):
                round_weight(w, g)
            for g in range(PASSES):
                quantize_weight(w, g)

        prepare(1)
        smooth_first()
        prepare(2)
        smooth(1)
        for c in range(BLOCKS):
            ratio(0, c)
        prepare(3)
        smooth(2)
        for c in range(BLOCKS):
            ratio(1, c)
        prepare(4)
        for c in range(BLOCKS):
            ratio(2, c)
        prepare(5)
        for c in range(BLOCKS):
            invert(c)
        for i in range(CANDS - 1):
            for c in range(BLOCKS):
                weigh(i, c)
        for c in range(BLOCKS):
            weigh(CANDS - 1, c)
            finish(c)
        nc.sync.dma_start(out=words_dram, in_=out_words[:].bitcast(I32))
        for quad in range(4):
            queue = nc.scalar if quad % 2 else nc.sync
            queue.dma_start(
                out=out_2[0, 4 * quad : 4 * quad + 4, :].bitcast(I32),
                in_=out_scales[32 * quad : 32 * quad + 4, :].bitcast(I32),
            )
